import numpy as np
import ml_dtypes


def mxq(x, axis, fmt="e4m3"):
    dtype, down = {"e4m3": (ml_dtypes.float8_e4m3fn, 7), "e5m2": (ml_dtypes.float8_e5m2, 14)}[fmt]
    v = np.moveaxis(np.asarray(x, np.float32).astype(ml_dtypes.bfloat16).astype(np.float64), axis, -1)
    blocks = v.reshape(v.shape[:-1] + (-1, 32))
    amax = np.abs(blocks).max(-1, keepdims=True)
    byte = np.maximum(np.where(amax > 0, np.frexp(amax)[1] - 1 + 127, 0) - down, 1)
    scale = np.exp2(byte - 127.0)
    codes = (blocks / scale).astype(np.float32).astype(dtype).astype(np.float64)
    return np.moveaxis((codes * scale).reshape(v.shape), -1, axis)


WIDE = False


def mx_kscale(k):
    if not WIDE:
        return np.ones(k)
    levels = np.array([10, -10, 5, -5, 0])
    if k % 512:
        return np.exp2(np.random.permutation(np.resize(levels, k // 32))).repeat(32)
    a = np.empty((k // 512, 16))
    for p in range(k // 512):
        a[p, :8] = np.random.permutation(np.resize(levels, 8))
        for g in range(8):
            far = levels[np.abs(levels - a[p, g]) >= 10]
            a[p, g + 8] = far[np.random.randint(len(far))]
    return np.exp2(a.ravel()).repeat(32)


def f64(x):
    return np.asarray(x).astype(np.float64)


def striped(idx):
    return np.tile(idx.reshape(-1, 16).T, (8, 1)).astype(np.uint16)


def unstriped(offs):
    return offs[:16].T.reshape(-1).astype(np.int64)


def striped8(idx):
    return np.concatenate([x.reshape(-1, 16).T for x in idx]).astype(np.uint16)


def runs(offs, k):
    lists = np.stack([offs[16 * r : 16 * r + 16].T.reshape(-1) for r in range(8)]).astype(np.int64)
    return lists[np.arange(k) % 512 // 64]


def pack_weight(w):
    k, n = w.shape
    w = f64(np.asarray(w, np.float32).astype(ml_dtypes.bfloat16)).reshape(k // 32, 32, n)
    amax = np.abs(w).max(1)
    byte = np.clip(np.where(amax > 0, np.frexp(amax)[1] - 1 + 127 - 7, 1), 1, 254)
    scaled = (w * np.exp2(127.0 - byte)[:, None, :]).reshape(k, n).astype(np.float32)
    words = np.ascontiguousarray(scaled.reshape(k // 512, 128, 4, n).transpose(0, 1, 3, 2)).astype(ml_dtypes.float8_e4m3fn).view(np.uint8)
    return words, np.ascontiguousarray(byte.astype(np.uint8).reshape(k // 512, 16, n))


def unpack_weight(words, scales):
    g, p, n, _ = words.shape
    vals = np.ascontiguousarray(words).view(ml_dtypes.float8_e4m3fn).astype(np.float64) * np.repeat(np.exp2(scales.astype(np.float64) - 127.0), 8, axis=1)[..., None]
    return vals.transpose(0, 1, 3, 2).reshape(g * 512, n)


def sigmoid(v):
    return 1.0 / (1.0 + np.exp(-np.maximum(v, -700.0)))


K, T, S, N, H, J = 512, 2048, 512, 512, 512, 512


def setup_inputs():
    n = np.random.standard_normal
    s = mx_kscale(K)[:, None]
    u = mx_kscale(H)
    packed_xT = pack_weight(n((K, T)) * s)
    return {
        "x_words": packed_xT[0],
        "x_scales": packed_xT[1],
        "w1": (n((K, H)) / np.sqrt(K) / s).astype(np.float32),
        "tab": n((H, J)).astype(np.float32),
        "gn": (np.random.uniform(0.5, 1.5, (H, 1)) * u[:, None]).astype(np.float32),
        "w2": (n((H, N)) / np.sqrt(H) / u[:, None]).astype(np.float32),
        "offs": striped(np.random.permutation(T)[:S]),
        "n1": striped8(np.random.randint(0, J, (8, S))),
        "n2": striped8(np.stack([np.random.permutation(S) for _ in range(8)])),
        "n3": striped8(np.stack([np.random.permutation(S) for _ in range(8)])),
        "n4": striped8(np.stack([np.random.permutation(S) for _ in range(8)])),
    }


def reference(x_words, x_scales, w1, tab, gn, w2, offs, n1, n2, n3, n4):
    xq = unpack_weight(x_words, x_scales)[:, unstriped(offs)]
    y = mxq(f64(w1), 0, "e4m3").T @ xq
    z = f64(gn) * (np.maximum(y + f64(tab)[np.arange(H)[:, None], runs(n1, H)], y[np.arange(H)[:, None], runs(n2, H)]))
    h = mxq(f64(w2), 0, "e4m3").T @ mxq(z, 0, "e4m3")
    return np.maximum(h * (sigmoid(h[np.arange(N)[:, None], runs(n3, N)])), h[np.arange(N)[:, None], runs(n4, N)])

@@ -1,0 +1,207 @@
+from contextlib import ExitStack
+
+import concourse.mybir as mybir
+
+K, T, S, N, H, J = 512, 2048, 512, 512, 512, 512
+FLOPS = 2 * K * H * S + 2 * H * N * S
+
+F32 = mybir.dt.float32
+BF16 = mybir.dt.bfloat16
+I32 = mybir.dt.int32
+U32 = mybir.dt.uint32
+U16 = mybir.dt.uint16
+U8 = mybir.dt.uint8
+FP8X4 = mybir.dt.float8_e4m3fn_x4
+ALU = mybir.AluOpType
+ACT = mybir.ActivationFunctionType
+
+P = 128
+PACK = 4
+HALF = S // 2
+QUARTER = S // 4
+
+
+def tile_picked_laykindgmax_none_p_kernel(tc, x_words, x_scales, w1, tab, gn, w2, offs, n1, n2, n3, n4, out):
+    nc = tc.nc
+    planes = range(PACK)
+
+    def entries(lst, a, b):
+        return lst[:, a // 16 : b // 16]
+
+    with ExitStack() as ctx:
+        keep = ctx.enter_context(tc.tile_pool(name="keep", bufs=1))
+        psum = ctx.enter_context(tc.psum_pool(name="psum", bufs=1))
+
+        offs_sb = keep.tile([P, S // 16], U16, name="offs_sb")
+        n1_sb = keep.tile([P, S // 16], U16, name="n1_sb")
+        n2_sb = keep.tile([P, S // 16], U16, name="n2_sb")
+        n3_sb = keep.tile([P, S // 16], U16, name="n3_sb")
+        n4_sb = keep.tile([P, S // 16], U16, name="n4_sb")
+
+        warm = keep.tile([P, 1], F32, name="warm")
+        warm_out = keep.tile([P, 1], F32, name="warm_out")
+        xs = keep.tile([P, T], U8, name="xs", align_bytes=64)
+        nc.vector.memset(xs[:].bitcast(I32), 0)
+        nc.vector.memset(warm[:], 0.0)
+        nc.scalar.activation(warm_out[:], warm[:], ACT.Sigmoid)
+
+        tab_rows = tab.rearrange("(p t) c -> p t c", t=PACK)
+        w1_rows = w1.rearrange("(p j) c -> p j c", j=PACK)
+        tab_sb = [keep.tile([P, J], F32, name=f"tab{t}") for t in planes]
+        w1_raw = [keep.tile([P, PACK, H // 2], F32, name=f"w1_raw{u}") for u in range(2)]
+        w2_raw = keep.tile([P, PACK, N], F32, name="w2_raw")
+        xw = keep.tile([P, T], I32, name="xw")
+        gn_sb = keep.tile([P, PACK], F32, name="gn_sb")
+
+        nc.sync.dma_start(n1_sb[:], n1)
+        for t in range(3):
+            nc.sync.dma_start(tab_sb[t][:], tab_rows[:, t, :])
+        nc.sync.dma_start(offs_sb[:], offs)
+        for u in range(2):
+            nc.sync.dma_start(w1_raw[u][:], w1_rows[:, :, u * (H // 2) : (u + 1) * (H // 2)])
+        nc.sync.dma_start(xw[:], x_words[0].rearrange("p n t -> p (n t)").bitcast(I32))
+        nc.sync.dma_start(n2_sb[:], n2)
+        nc.sync.dma_start(tab_sb[3][:], tab_rows[:, 3, :])
+        nc.sync.dma_start(w2_raw[:], w2.rearrange("(p j) c -> p j c", j=PACK))
+        nc.sync.dma_start(n3_sb[:], n3)
+        nc.sync.dma_start(n4_sb[:], n4)
+        for q in range(4):
+            nc.scalar.dma_start(xs[32 * q : 32 * q + 4, :].bitcast(I32), x_scales[0, 4 * q : 4 * q + 4, :].bitcast(I32))
+        nc.gpsimd.dma_start(gn_sb[:], gn.rearrange("(p t) o -> p (t o)", t=PACK))
+
+        step = keep.tile([P, PACK], F32, name="step")
+        sgn = keep.tile([P, PACK], F32, name="sgn")
+        gain = keep.tile([P, PACK], F32, name="gain")
+        nc.gpsimd.tensor_scalar(step[:], gn_sb[:], 0.0, 2.0, ALU.is_ge, ALU.mult)
+        nc.gpsimd.tensor_scalar(sgn[:], step[:], 1.0, -1.0, ALU.mult, ALU.add)
+        nc.gpsimd.tensor_tensor(gain[:], gn_sb[:], sgn[:], ALU.mult)
+
+        w1_bf = keep.tile([P, PACK, P, PACK], BF16, name="w1_bf", align_bytes=64)
+        for u in range(2):
+            nc.scalar.copy(
+                w1_bf[:, :, u * (P // 2) : (u + 1) * (P // 2), :].rearrange("p t m j -> p m j t"),
+                w1_raw[u][:].rearrange("p j (m t) -> p m j t", t=PACK),
+            )
+
+        tg = [keep.tile([P, S], F32, name=f"tg{t}") for t in planes]
+
+        def gather_tab(t):
+            for a in (0, HALF):
+                nc.vector.tensor_copy(tg[t][:, a : a + HALF], tab_sb[t][:].indirect(entries(n1_sb, a, a + HALF)))
+
+        for t in range(3):
+            gather_tab(t)
+        x_sc = keep.tile([P, S], U8, name="x_sc", align_bytes=64)
+        x_cd = keep.tile([P, S], U32, name="x_cd", align_bytes=64)
+        nc.vector.tensor_copy(x_sc[:], xs[:].indirect(offs_sb[:]))
+        w1_cd = keep.tile([P, H], U32, name="w1_cd", align_bytes=64)
+        w1_sc = keep.tile([P, H], U8, name="w1_sc", align_bytes=64)
+        nc.vector.quantize_mx(w1_cd[:].bitcast(FP8X4), w1_sc[:], w1_bf[:].rearrange("p t m j -> p (t m j)"))
+        nc.vector.tensor_copy(x_cd[:], xw[:].bitcast(U32).indirect(offs_sb[:]))
+        gather_tab(3)
+
+        y_ps = [psum.tile([P, S], F32, name=f"y_ps{t}") for t in planes]
+        gy = [keep.tile([P, S], F32, name=f"gy{t}") for t in planes]
+        for t in planes:
+            nc.tensor.matmul_mx(
+                y_ps[t][:], w1_cd[:, t * P : (t + 1) * P].bitcast(FP8X4), w1_sc[:, t * P : (t + 1) * P],
+                x_cd[:].bitcast(FP8X4), x_sc[:], start=True, stop=True,
+            )
+            nc.scalar.activation(gy[t][:], y_ps[t][:], ACT.Copy, scale=gain[:, t : t + 1])
+
+        w2_sg = keep.tile([P, PACK, N], BF16, name="w2_sg")
+        w2_bf = keep.tile([P, PACK, P, PACK], BF16, name="w2_bf", align_bytes=64)
+        for j in planes:
+            nc.scalar.activation(w2_sg[:, j, :], w2_raw[:, j, :], ACT.Copy, scale=sgn[:, j : j + 1])
+        nc.scalar.copy(w2_bf[:].rearrange("p t m j -> p m j t"), w2_sg[:].rearrange("p j (m t) -> p m j t", t=PACK))
+        w2_cd = keep.tile([P, N], U32, name="w2_cd", align_bytes=64)
+        w2_sc = keep.tile([P, N], U8, name="w2_sc", align_bytes=64)
+
+        first = keep.tile([P, PACK, S], F32, name="first")
+        second = keep.tile([P, PACK, S], F32, name="second")
+        pieces = [(0, HALF), (HALF, HALF + QUARTER), (HALF + QUARTER, S)]
+        z_bf = [keep.tile([P, b - a, PACK], BF16, name=f"z_bf{a}", align_bytes=64) for a, b in pieces]
+        z_cd = [keep.tile([P, b - a], U32, name=f"z_cd{a}", align_bytes=64) for a, b in pieces]
+        z_sc = [keep.tile([P, b - a], U8, name=f"z_sc{a}", align_bytes=64) for a, b in pieces]
+        h_ps = [psum.tile([P, S], F32, name=f"h_ps{t}") for t in planes]
+        h_sb = [keep.tile([P, S], F32, name=f"h_sb{t}") for t in planes]
+
+        def gather_y(t, a):
+            nc.vector.tensor_copy(second[:, t, a : a + HALF], gy[t][:].indirect(entries(n2_sb, a, a + HALF)))
+
+        def larger(i):
+            a, b = pieces[i]
+            nc.vector.tensor_tensor(
+                z_bf[i][:].rearrange("p (c i) t -> p c t i", i=2),
+                first[:, :, a:b].rearrange("p t (c i) -> p c t i", i=2),
+                second[:, :, a:b].rearrange("p t (c i) -> p c t i", i=2),
+                ALU.max,
+            )
+
+        def quantise_z(i):
+            nc.vector.quantize_mx(z_cd[i][:].bitcast(FP8X4), z_sc[i][:], z_bf[i][:].rearrange("p c t -> p (c t)"))
+
+        def second_product(i):
+            a, b = pieces[i]
+            for t in planes:
+                nc.tensor.matmul_mx(
+                    h_ps[t][:, a:b], w2_cd[:, t * P : (t + 1) * P].bitcast(FP8X4), w2_sc[:, t * P : (t + 1) * P],
+                    z_cd[i][:].bitcast(FP8X4), z_sc[i][:], start=True, stop=True,
+                )
+
+        for t in planes:
+            gather_y(t, 0)
+            nc.vector.scalar_tensor_tensor(first[:, t, :], tg[t][:], gain[:, t : t + 1], gy[t][:], ALU.mult, ALU.add)
+        gather_y(0, HALF)
+        larger(0)
+        gather_y(1, HALF)
+        quantise_z(0)
+        gather_y(2, HALF)
+        gather_y(3, HALF)
+        nc.vector.quantize_mx(w2_cd[:].bitcast(FP8X4), w2_sc[:], w2_bf[:].rearrange("p t m j -> p (t m j)"))
+        second_product(0)
+        for t in planes:
+            nc.scalar.copy(h_sb[t][:, :HALF], h_ps[t][:, :HALF])
+        larger(1)
+        larger(2)
+        quantise_z(1)
+        quantise_z(2)
+        second_product(1)
+        second_product(2)
+        for t in planes:
+            nc.scalar.copy(h_sb[t][:, HALF:], h_ps[t][:, HALF:])
+
+        out_rows = out.rearrange("(p t) c -> p t c", t=PACK)
+        gate = [keep.tile([P, S], F32, name=f"gate{t}") for t in planes]
+        other = [keep.tile([P, S], F32, name=f"other{t}") for t in planes]
+        gated = [keep.tile([P, S], F32, name=f"gated{t}") for t in planes]
+        res = [keep.tile([P, S], F32, name=f"res{t}") for t in planes]
+        for t in planes:
+            for a in (0, HALF):
+                nc.scalar.activation(gate[t][:, a : a + HALF], h_sb[t][:].indirect(entries(n3_sb, a, a + HALF)), ACT.Sigmoid)
+
+        def gather_h(t):
+            for a in (0, HALF):
+                nc.vector.tensor_copy(other[t][:, a : a + HALF], h_sb[t][:].indirect(entries(n4_sb, a, a + HALF)))
+
+        def times_gate(t, a, b):
+            nc.vector.tensor_tensor(gated[t][:, a:b], h_ps[t][:, a:b], gate[t][:, a:b], ALU.mult)
+
+        def finish(t, a, b):
+            nc.vector.tensor_tensor(res[t][:, a:b], gated[t][:, a:b], other[t][:, a:b], ALU.max)
+            nc.sync.dma_start(out_rows[:, t, a:b], res[t][:, a:b])
+
+        gather_h(0)
+        gather_h(1)
+        times_gate(0, 0, S)
+        gather_h(2)
+        finish(0, 0, S)
+        times_gate(1, 0, S)
+        gather_h(3)
+        finish(1, 0, S)
+        times_gate(2, 0, S)
+        times_gate(3, 0, HALF)
+        finish(2, 0, S)
+        times_gate(3, HALF, S)
+        finish(3, 0, HALF)
+        finish(3, HALF, S)

@@ -47,26 +47,29 @@ def tile_picked_laykindgmax_none_p_kernel(tc, x_words, x_scales, w1, tab, gn, w2
 
         tab_rows = tab.rearrange("(p t) c -> p t c", t=PACK)
         w1_rows = w1.rearrange("(p j) c -> p j c", j=PACK)
-        tab_sb = [keep.tile([P, J], F32, name=f"tab{t}") for t in planes]
+        w2_rows = w2.rearrange("(p j) c -> p j c", j=PACK)
+        tab_sb = [keep.tile([P, 2 * J], F32, name=f"tab{t}") for t in planes]
         w1_raw = [keep.tile([P, PACK, H // 2], F32, name=f"w1_raw{u}") for u in range(2)]
-        w2_raw = keep.tile([P, PACK, N], F32, name="w2_raw")
+        w2_raw = [keep.tile([P, N], F32, name=f"w2_raw{j}") for j in planes]
         xw = keep.tile([P, T], I32, name="xw")
         gn_sb = keep.tile([P, PACK], F32, name="gn_sb")
 
         nc.sync.dma_start(n1_sb[:], n1)
         for t in range(3):
-            nc.sync.dma_start(tab_sb[t][:], tab_rows[:, t, :])
-        nc.sync.dma_start(offs_sb[:], offs)
+            nc.sync.dma_start(tab_sb[t][:, :J], tab_rows[:, t, :])
         for u in range(2):
             nc.sync.dma_start(w1_raw[u][:], w1_rows[:, :, u * (H // 2) : (u + 1) * (H // 2)])
+        nc.sync.dma_start(offs_sb[:], offs)
         nc.sync.dma_start(xw[:], x_words[0].rearrange("p n t -> p (n t)").bitcast(I32))
         nc.sync.dma_start(n2_sb[:], n2)
-        nc.sync.dma_start(tab_sb[3][:], tab_rows[:, 3, :])
-        nc.sync.dma_start(w2_raw[:], w2.rearrange("(p j) c -> p j c", j=PACK))
+        nc.sync.dma_start(tab_sb[3][:, :J], tab_rows[:, 3, :])
+        for j in planes:
+            nc.sync.dma_start(w2_raw[j][:], w2_rows[:, j, :])
         nc.sync.dma_start(n3_sb[:], n3)
         nc.sync.dma_start(n4_sb[:], n4)
         for q in range(4):
-            nc.scalar.dma_start(xs[32 * q : 32 * q + 4, :].bitcast(I32), x_scales[0, 4 * q : 4 * q + 4, :].bitcast(I32))
+            queue = nc.gpsimd if q < 1 else nc.scalar
+            queue.dma_start(xs[32 * q : 32 * q + 4, :].bitcast(I32), x_scales[0, 4 * q : 4 * q + 4, :].bitcast(I32))
         nc.gpsimd.dma_start(gn_sb[:], gn.rearrange("(p t) o -> p (t o)", t=PACK))
 
         step = keep.tile([P, PACK], F32, name="step")
@@ -84,13 +87,17 @@ def tile_picked_laykindgmax_none_p_kernel(tc, x_words, x_scales, w1, tab, gn, w2
             )
 
         tg = [keep.tile([P, S], F32, name=f"tg{t}") for t in planes]
+        gtg = [keep.tile([P, S], F32, name=f"gtg{t}") for t in planes]
 
         def gather_tab(t):
-            for a in (0, HALF):
-                nc.vector.tensor_copy(tg[t][:, a : a + HALF], tab_sb[t][:].indirect(entries(n1_sb, a, a + HALF)))
+            nc.vector.tensor_copy(tg[t][:], tab_sb[t][:].indirect(n1_sb[:]))
+
+        def scale_tab(t):
+            nc.scalar.activation(gtg[t][:], tg[t][:], ACT.Copy, scale=gain[:, t : t + 1])
 
         for t in range(3):
             gather_tab(t)
+            scale_tab(t)
         x_sc = keep.tile([P, S], U8, name="x_sc", align_bytes=64)
         x_cd = keep.tile([P, S], U32, name="x_cd", align_bytes=64)
         nc.vector.tensor_copy(x_sc[:], xs[:].indirect(offs_sb[:]))
@@ -101,18 +108,21 @@ def tile_picked_laykindgmax_none_p_kernel(tc, x_words, x_scales, w1, tab, gn, w2
         gather_tab(3)
 
         y_ps = [psum.tile([P, S], F32, name=f"y_ps{t}") for t in planes]
-        gy = [keep.tile([P, S], F32, name=f"gy{t}") for t in planes]
+        gy = [keep.tile([P, 2 * S], F32, name=f"gy{t}") for t in planes]
         for t in planes:
             nc.tensor.matmul_mx(
                 y_ps[t][:], w1_cd[:, t * P : (t + 1) * P].bitcast(FP8X4), w1_sc[:, t * P : (t + 1) * P],
                 x_cd[:].bitcast(FP8X4), x_sc[:], start=True, stop=True,
             )
-            nc.scalar.activation(gy[t][:], y_ps[t][:], ACT.Copy, scale=gain[:, t : t + 1])
+            nc.scalar.activation(gy[t][:, :S], y_ps[t][:], ACT.Copy, scale=gain[:, t : t + 1])
+        scale_tab(3)
 
         w2_sg = keep.tile([P, PACK, N], BF16, name="w2_sg")
-        w2_bf = keep.tile([P, PACK, P, PACK], BF16, name="w2_bf", align_bytes=64)
-        for j in planes:
-            nc.scalar.activation(w2_sg[:, j, :], w2_raw[:, j, :], ACT.Copy, scale=sgn[:, j : j + 1])
+        w2_bf = keep.tile([P, PACK, P, PACK], BF16, name="w2_bf", tag="w2_bf", align_bytes=64)
+        for j in range(2):
+            nc.gpsimd.tensor_scalar(w2_sg[:, j, :], w2_raw[j][:], sgn[:, j : j + 1], 0.0, ALU.mult, ALU.add)
+        for j in range(2, PACK):
+            nc.scalar.activation(w2_sg[:, j, :], w2_raw[j][:], ACT.Copy, scale=sgn[:, j : j + 1])
         nc.scalar.copy(w2_bf[:].rearrange("p t m j -> p m j t"), w2_sg[:].rearrange("p j (m t) -> p m j t", t=PACK))
         w2_cd = keep.tile([P, N], U32, name="w2_cd", align_bytes=64)
         w2_sc = keep.tile([P, N], U8, name="w2_sc", align_bytes=64)
@@ -120,17 +130,15 @@ def tile_picked_laykindgmax_none_p_kernel(tc, x_words, x_scales, w1, tab, gn, w2
         first = keep.tile([P, PACK, S], F32, name="first")
         second = keep.tile([P, PACK, S], F32, name="second")
         pieces = [(0, HALF), (HALF, HALF + QUARTER), (HALF + QUARTER, S)]
-        z_bf = [keep.tile([P, b - a, PACK], BF16, name=f"z_bf{a}", align_bytes=64) for a, b in pieces]
+        z_bf = {}
         z_cd = [keep.tile([P, b - a], U32, name=f"z_cd{a}", align_bytes=64) for a, b in pieces]
         z_sc = [keep.tile([P, b - a], U8, name=f"z_sc{a}", align_bytes=64) for a, b in pieces]
         h_ps = [psum.tile([P, S], F32, name=f"h_ps{t}") for t in planes]
-        h_sb = [keep.tile([P, S], F32, name=f"h_sb{t}") for t in planes]
-
-        def gather_y(t, a):
-            nc.vector.tensor_copy(second[:, t, a : a + HALF], gy[t][:].indirect(entries(n2_sb, a, a + HALF)))
+        h_sb = [keep.tile([P, 2 * S], F32, name=f"h_sb{t}") for t in planes]
 
         def larger(i):
             a, b = pieces[i]
+            z_bf[i] = keep.tile([P, b - a, PACK], BF16, name=f"z_bf{i}", tag=("w2_bf" if i == 1 else f"z_bf{i}"), align_bytes=64)
             nc.vector.tensor_tensor(
                 z_bf[i][:].rearrange("p (c i) t -> p c t i", i=2),
                 first[:, :, a:b].rearrange("p t (c i) -> p c t i", i=2),
@@ -141,51 +149,55 @@ def tile_picked_laykindgmax_none_p_kernel(tc, x_words, x_scales, w1, tab, gn, w2
         def quantise_z(i):
             nc.vector.quantize_mx(z_cd[i][:].bitcast(FP8X4), z_sc[i][:], z_bf[i][:].rearrange("p c t -> p (c t)"))
 
-        def second_product(i):
+        def second_product(i, t):
             a, b = pieces[i]
-            for t in planes:
-                nc.tensor.matmul_mx(
-                    h_ps[t][:, a:b], w2_cd[:, t * P : (t + 1) * P].bitcast(FP8X4), w2_sc[:, t * P : (t + 1) * P],
-                    z_cd[i][:].bitcast(FP8X4), z_sc[i][:], start=True, stop=True,
-                )
+            nc.tensor.matmul_mx(
+                h_ps[t][:, a:b], w2_cd[:, t * P : (t + 1) * P].bitcast(FP8X4), w2_sc[:, t * P : (t + 1) * P],
+                z_cd[i][:].bitcast(FP8X4), z_sc[i][:], start=True, stop=True,
+            )
 
         for t in planes:
-            gather_y(t, 0)
-            nc.vector.scalar_tensor_tensor(first[:, t, :], tg[t][:], gain[:, t : t + 1], gy[t][:], ALU.mult, ALU.add)
-        gather_y(0, HALF)
+            nc.vector.tensor_copy(second[:, t, :], gy[t][:].indirect(n2_sb[:]))
+            nc.gpsimd.tensor_tensor(first[:, t, :], gtg[t][:], gy[t][:, :S], ALU.add)
         larger(0)
-        gather_y(1, HALF)
-        quantise_z(0)
-        gather_y(2, HALF)
-        gather_y(3, HALF)
         nc.vector.quantize_mx(w2_cd[:].bitcast(FP8X4), w2_sc[:], w2_bf[:].rearrange("p t m j -> p (t m j)"))
-        second_product(0)
+        quantise_z(0)
         for t in planes:
+            second_product(0, t)
             nc.scalar.copy(h_sb[t][:, :HALF], h_ps[t][:, :HALF])
         larger(1)
         larger(2)
         quantise_z(1)
         quantise_z(2)
-        second_product(1)
-        second_product(2)
         for t in planes:
-            nc.scalar.copy(h_sb[t][:, HALF:], h_ps[t][:, HALF:])
+            second_product(1, t)
+        for t in planes:
+            second_product(2, t)
 
         out_rows = out.rearrange("(p t) c -> p t c", t=PACK)
         gate = [keep.tile([P, S], F32, name=f"gate{t}") for t in planes]
         other = [keep.tile([P, S], F32, name=f"other{t}") for t in planes]
         gated = [keep.tile([P, S], F32, name=f"gated{t}") for t in planes]
         res = [keep.tile([P, S], F32, name=f"res{t}") for t in planes]
-        for t in planes:
-            for a in (0, HALF):
-                nc.scalar.activation(gate[t][:, a : a + HALF], h_sb[t][:].indirect(entries(n3_sb, a, a + HALF)), ACT.Sigmoid)
+
+        def gather_gate(t, a, b):
+            nc.scalar.activation(gate[t][:, a:b], h_sb[t][:].indirect(entries(n3_sb, a, b)), ACT.Sigmoid)
+
+        nc.vector.tensor_copy(h_sb[0][:, HALF:S], h_ps[0][:, HALF:])
+        for t in range(3):
+            nc.scalar.copy(h_sb[t + 1][:, HALF:S], h_ps[t + 1][:, HALF:])
+            gather_gate(t, 0, S)
+        gather_gate(3, 0, HALF)
+        gather_gate(3, HALF, S)
 
         def gather_h(t):
-            for a in (0, HALF):
-                nc.vector.tensor_copy(other[t][:, a : a + HALF], h_sb[t][:].indirect(entries(n4_sb, a, a + HALF)))
+            nc.vector.tensor_copy(other[t][:], h_sb[t][:].indirect(n4_sb[:]))
 
         def times_gate(t, a, b):
-            nc.vector.tensor_tensor(gated[t][:, a:b], h_ps[t][:, a:b], gate[t][:, a:b], ALU.mult)
+            if t < 3:
+                nc.gpsimd.tensor_tensor(gated[t][:, a:b], h_sb[t][:, a:b], gate[t][:, a:b], ALU.mult)
+            else:
+                nc.vector.tensor_tensor(gated[t][:, a:b], h_ps[t][:, a:b], gate[t][:, a:b], ALU.mult)
 
         def finish(t, a, b):
             nc.vector.tensor_tensor(res[t][:, a:b], gated[t][:, a:b], other[t][:, a:b], ALU.max)
@@ -194,11 +206,11 @@ def tile_picked_laykindgmax_none_p_kernel(tc, x_words, x_scales, w1, tab, gn, w2
         gather_h(0)
         gather_h(1)
         times_gate(0, 0, S)
-        gather_h(2)
         finish(0, 0, S)
+        gather_h(2)
         times_gate(1, 0, S)
-        gather_h(3)
         finish(1, 0, S)
+        gather_h(3)
         times_gate(2, 0, S)
         times_gate(3, 0, HALF)
         finish(2, 0, S)

from contextlib import ExitStack

import concourse.mybir as mybir

K, T, S, N, H, J = 512, 2048, 512, 512, 512, 512
FLOPS = 2 * K * H * S + 2 * H * N * S

F32 = mybir.dt.float32
BF16 = mybir.dt.bfloat16
I32 = mybir.dt.int32
U32 = mybir.dt.uint32
U16 = mybir.dt.uint16
U8 = mybir.dt.uint8
FP8X4 = mybir.dt.float8_e4m3fn_x4
ALU = mybir.AluOpType
ACT = mybir.ActivationFunctionType

P = 128
PACK = 4
HALF = S // 2
QUARTER = S // 4


def tile_picked_laykindgmax_none_p_kernel(tc, x_words, x_scales, w1, tab, gn, w2, offs, n1, n2, n3, n4, out):
    nc = tc.nc
    planes = range(PACK)

    def entries(lst, a, b):
        return lst[:, a // 16 : b // 16]

    with ExitStack() as ctx:
        keep = ctx.enter_context(tc.tile_pool(name="keep", bufs=1))
        psum = ctx.enter_context(tc.psum_pool(name="psum", bufs=1))

        offs_sb = keep.tile([P, S // 16], U16, name="offs_sb")
        n1_sb = keep.tile([P, S // 16], U16, name="n1_sb")
        n2_sb = keep.tile([P, S // 16], U16, name="n2_sb")
        n3_sb = keep.tile([P, S // 16], U16, name="n3_sb")
        n4_sb = keep.tile([P, S // 16], U16, name="n4_sb")

        warm = keep.tile([P, 1], F32, name="warm")
        warm_out = keep.tile([P, 1], F32, name="warm_out")
        xs = keep.tile([P, T], U8, name="xs", align_bytes=64)
        nc.vector.memset(xs[:].bitcast(I32), 0)
        nc.vector.memset(warm[:], 0.0)
        nc.scalar.activation(warm_out[:], warm[:], ACT.Sigmoid)

        tab_rows = tab.rearrange("(p t) c -> p t c", t=PACK)
        w1_rows = w1.rearrange("(p j) c -> p j c", j=PACK)
        w2_rows = w2.rearrange("(p j) c -> p j c", j=PACK)
        tab_sb = [keep.tile([P, 2 * J], F32, name=f"tab{t}") for t in planes]
        w1_raw = [keep.tile([P, PACK, H // 2], F32, name=f"w1_raw{u}") for u in range(2)]
        w2_raw = [keep.tile([P, N], F32, name=f"w2_raw{j}") for j in planes]
        xw = keep.tile([P, T], I32, name="xw")
        gn_sb = keep.tile([P, PACK], F32, name="gn_sb")

        nc.sync.dma_start(n1_sb[:], n1)
        for t in range(3):
            nc.sync.dma_start(tab_sb[t][:, :J], tab_rows[:, t, :])
        for u in range(2):
            nc.sync.dma_start(w1_raw[u][:], w1_rows[:, :, u * (H // 2) : (u + 1) * (H // 2)])
        nc.sync.dma_start(offs_sb[:], offs)
        nc.sync.dma_start(xw[:], x_words[0].rearrange("p n t -> p (n t)").bitcast(I32))
        nc.sync.dma_start(n2_sb[:], n2)
        nc.sync.dma_start(tab_sb[3][:, :J], tab_rows[:, 3, :])
        for j in planes:
            nc.sync.dma_start(w2_raw[j][:], w2_rows[:, j, :])
        nc.sync.dma_start(n3_sb[:], n3)
        nc.sync.dma_start(n4_sb[:], n4)
        for q in range(4):
            queue = nc.gpsimd if q < 1 else nc.scalar
            queue.dma_start(xs[32 * q : 32 * q + 4, :].bitcast(I32), x_scales[0, 4 * q : 4 * q + 4, :].bitcast(I32))
        nc.gpsimd.dma_start(gn_sb[:], gn.rearrange("(p t) o -> p (t o)", t=PACK))

        step = keep.tile([P, PACK], F32, name="step")
        sgn = keep.tile([P, PACK], F32, name="sgn")
        gain = keep.tile([P, PACK], F32, name="gain")
        nc.gpsimd.tensor_scalar(step[:], gn_sb[:], 0.0, 2.0, ALU.is_ge, ALU.mult)
        nc.gpsimd.tensor_scalar(sgn[:], step[:], 1.0, -1.0, ALU.mult, ALU.add)
        nc.gpsimd.tensor_tensor(gain[:], gn_sb[:], sgn[:], ALU.mult)

        w1_bf = keep.tile([P, PACK, P, PACK], BF16, name="w1_bf", align_bytes=64)
        for u in range(2):
            nc.scalar.copy(
                w1_bf[:, :, u * (P // 2) : (u + 1) * (P // 2), :].rearrange("p t m j -> p m j t"),
                w1_raw[u][:].rearrange("p j (m t) -> p m j t", t=PACK),
            )

        tg = [keep.tile([P, S], F32, name=f"tg{t}") for t in planes]
        gtg = [keep.tile([P, S], F32, name=f"gtg{t}") for t in planes]

        def gather_tab(t):
            nc.vector.tensor_copy(tg[t][:], tab_sb[t][:].indirect(n1_sb[:]))

        def scale_tab(t):
            nc.scalar.activation(gtg[t][:], tg[t][:], ACT.Copy, scale=gain[:, t : t + 1])

        for t in range(3):
            gather_tab(t)
            scale_tab(t)
        x_sc = keep.tile([P, S], U8, name="x_sc", align_bytes=64)
        x_cd = keep.tile([P, S], U32, name="x_cd", align_bytes=64)
        nc.vector.tensor_copy(x_sc[:], xs[:].indirect(offs_sb[:]))
        w1_cd = keep.tile([P, H], U32, name="w1_cd", align_bytes=64)
        w1_sc = keep.tile([P, H], U8, name="w1_sc", align_bytes=64)
        nc.vector.quantize_mx(w1_cd[:].bitcast(FP8X4), w1_sc[:], w1_bf[:].rearrange("p t m j -> p (t m j)"))
        nc.vector.tensor_copy(x_cd[:], xw[:].bitcast(U32).indirect(offs_sb[:]))
        gather_tab(3)

        y_ps = [psum.tile([P, S], F32, name=f"y_ps{t}") for t in planes]
        gy = [keep.tile([P, 2 * S], F32, name=f"gy{t}") for t in planes]
        for t in planes:
            nc.tensor.matmul_mx(
                y_ps[t][:], w1_cd[:, t * P : (t + 1) * P].bitcast(FP8X4), w1_sc[:, t * P : (t + 1) * P],
                x_cd[:].bitcast(FP8X4), x_sc[:], start=True, stop=True,
            )
            nc.scalar.activation(gy[t][:, :S], y_ps[t][:], ACT.Copy, scale=gain[:, t : t + 1])
        scale_tab(3)

        w2_sg = keep.tile([P, PACK, N], BF16, name="w2_sg")
        w2_bf = keep.tile([P, PACK, P, PACK], BF16, name="w2_bf", tag="w2_bf", align_bytes=64)
        for j in range(2):
            nc.gpsimd.tensor_scalar(w2_sg[:, j, :], w2_raw[j][:], sgn[:, j : j + 1], 0.0, ALU.mult, ALU.add)
        for j in range(2, PACK):
            nc.scalar.activation(w2_sg[:, j, :], w2_raw[j][:], ACT.Copy, scale=sgn[:, j : j + 1])
        nc.scalar.copy(w2_bf[:].rearrange("p t m j -> p m j t"), w2_sg[:].rearrange("p j (m t) -> p m j t", t=PACK))
        w2_cd = keep.tile([P, N], U32, name="w2_cd", align_bytes=64)
        w2_sc = keep.tile([P, N], U8, name="w2_sc", align_bytes=64)

        first = keep.tile([P, PACK, S], F32, name="first")
        second = keep.tile([P, PACK, S], F32, name="second")
        pieces = [(0, HALF), (HALF, HALF + QUARTER), (HALF + QUARTER, S)]
        z_bf = {}
        z_cd = [keep.tile([P, b - a], U32, name=f"z_cd{a}", align_bytes=64) for a, b in pieces]
        z_sc = [keep.tile([P, b - a], U8, name=f"z_sc{a}", align_bytes=64) for a, b in pieces]
        h_ps = [psum.tile([P, S], F32, name=f"h_ps{t}") for t in planes]
        h_sb = [keep.tile([P, 2 * S], F32, name=f"h_sb{t}") for t in planes]

        def larger(i):
            a, b = pieces[i]
            z_bf[i] = keep.tile([P, b - a, PACK], BF16, name=f"z_bf{i}", tag=("w2_bf" if i == 1 else f"z_bf{i}"), align_bytes=64)
            nc.vector.tensor_tensor(
                z_bf[i][:].rearrange("p (c i) t -> p c t i", i=2),
                first[:, :, a:b].rearrange("p t (c i) -> p c t i", i=2),
                second[:, :, a:b].rearrange("p t (c i) -> p c t i", i=2),
                ALU.max,
            )

        def quantise_z(i):
            nc.vector.quantize_mx(z_cd[i][:].bitcast(FP8X4), z_sc[i][:], z_bf[i][:].rearrange("p c t -> p (c t)"))

        def second_product(i, t):
            a, b = pieces[i]
            nc.tensor.matmul_mx(
                h_ps[t][:, a:b], w2_cd[:, t * P : (t + 1) * P].bitcast(FP8X4), w2_sc[:, t * P : (t + 1) * P],
                z_cd[i][:].bitcast(FP8X4), z_sc[i][:], start=True, stop=True,
            )

        for t in planes:
            nc.vector.tensor_copy(second[:, t, :], gy[t][:].indirect(n2_sb[:]))
            nc.gpsimd.tensor_tensor(first[:, t, :], gtg[t][:], gy[t][:, :S], ALU.add)
        larger(0)
        nc.vector.quantize_mx(w2_cd[:].bitcast(FP8X4), w2_sc[:], w2_bf[:].rearrange("p t m j -> p (t m j)"))
        quantise_z(0)
        for t in planes:
            second_product(0, t)
            nc.scalar.copy(h_sb[t][:, :HALF], h_ps[t][:, :HALF])
        larger(1)
        larger(2)
        quantise_z(1)
        quantise_z(2)
        for t in planes:
            second_product(1, t)
        for t in planes:
            second_product(2, t)

        out_rows = out.rearrange("(p t) c -> p t c", t=PACK)
        gate = [keep.tile([P, S], F32, name=f"gate{t}") for t in planes]
        other = [keep.tile([P, S], F32, name=f"other{t}") for t in planes]
        gated = [keep.tile([P, S], F32, name=f"gated{t}") for t in planes]
        res = [keep.tile([P, S], F32, name=f"res{t}") for t in planes]

        def gather_gate(t, a, b):
            nc.scalar.activation(gate[t][:, a:b], h_sb[t][:].indirect(entries(n3_sb, a, b)), ACT.Sigmoid)

        nc.vector.tensor_copy(h_sb[0][:, HALF:S], h_ps[0][:, HALF:])
        for t in range(3):
            nc.scalar.copy(h_sb[t + 1][:, HALF:S], h_ps[t + 1][:, HALF:])
            gather_gate(t, 0, S)
        gather_gate(3, 0, HALF)
        gather_gate(3, HALF, S)

        def gather_h(t):
            nc.vector.tensor_copy(other[t][:], h_sb[t][:].indirect(n4_sb[:]))

        def times_gate(t, a, b):
            if t < 3:
                nc.gpsimd.tensor_tensor(gated[t][:, a:b], h_sb[t][:, a:b], gate[t][:, a:b], ALU.mult)
            else:
                nc.vector.tensor_tensor(gated[t][:, a:b], h_ps[t][:, a:b], gate[t][:, a:b], ALU.mult)

        def finish(t, a, b):
            nc.vector.tensor_tensor(res[t][:, a:b], gated[t][:, a:b], other[t][:, a:b], ALU.max)
            nc.sync.dma_start(out_rows[:, t, a:b], res[t][:, a:b])

        gather_h(0)
        gather_h(1)
        times_gate(0, 0, S)
        finish(0, 0, S)
        gather_h(2)
        times_gate(1, 0, S)
        finish(1, 0, S)
        gather_h(3)
        times_gate(2, 0, S)
        times_gate(3, 0, HALF)
        finish(2, 0, S)
        times_gate(3, HALF, S)
        finish(3, 0, HALF)
        finish(3, HALF, S)
